import numpy as np
import ml_dtypes


def mxq(x, axis, fmt="e4m3"):
    dtype, down = {"e4m3": (ml_dtypes.float8_e4m3fn, 7), "e5m2": (ml_dtypes.float8_e5m2, 14)}[fmt]
    v = np.moveaxis(np.asarray(x, np.float32).astype(ml_dtypes.bfloat16).astype(np.float64), axis, -1)
    blocks = v.reshape(v.shape[:-1] + (-1, 32))
    amax = np.abs(blocks).max(-1, keepdims=True)
    byte = np.maximum(np.where(amax > 0, np.frexp(amax)[1] - 1 + 127, 0) - down, 1)
    scale = np.exp2(byte - 127.0)
    codes = (blocks / scale).astype(np.float32).astype(dtype).astype(np.float64)
    return np.moveaxis((codes * scale).reshape(v.shape), -1, axis)


WIDE = False


def mx_kscale(k):
    if not WIDE:
        return np.ones(k)
    levels = np.array([24, -24, 12, -12, 0])
    if k % 512:
        return np.exp2(np.random.permutation(np.resize(levels, k // 32))).repeat(32)
    a = np.empty((k // 512, 16))
    for p in range(k // 512):
        a[p, :8] = np.random.permutation(np.resize(levels, 8))
        for g in range(8):
            far = levels[np.abs(levels - a[p, g]) >= 10]
            a[p, g + 8] = far[np.random.randint(len(far))]
    return np.exp2(a.ravel()).repeat(32)


def f64(x):
    return np.asarray(x).astype(np.float64)


def striped8(idx):
    return np.concatenate([v.reshape(-1, 16).T for v in idx]).astype(np.uint16)


def unstriped8(offs):
    return np.stack([offs[16 * g:16 * g + 16].T.reshape(-1) for g in range(8)]).astype(np.int64)


K, N, T, J = 512, 512, 2048, 512


def setup_inputs():
    n = np.random.standard_normal
    s = mx_kscale(K)[:, None]
    return {
        "xT": (n((K, T)) * s).astype(np.float32),
        "wgt": np.repeat(np.random.uniform(0.5, 2.0, (8, 3 * J)), 16, axis=0).astype(np.float32),
        "w": (n((K, N)) / np.sqrt(K) / s).astype(np.float32),
        "iw0": (np.random.uniform(0.1, 0.9, (N, J))).astype(np.float32),
        "iw1": (np.random.uniform(0.1, 0.9, (N, J))).astype(np.float32),
        "iw2": (np.random.uniform(0.1, 0.9, (N, J))).astype(np.float32),
        "b": (0.3 * n(N)).astype(np.float32),
        "offs": striped8(np.stack([np.concatenate([np.random.permutation(T)[:J] for _ in range(3)]) for _ in range(8)])),
    }


def reference(xT, wgt, w, iw0, iw1, iw2, b, offs):
    idx = unstriped8(offs)
    rows = np.arange(K)
    xg = f64(wgt)[rows // 4 % 128] * f64(xT)[rows[:, None], idx[rows % 512 // 64]]
    xT_ = mxq(xg, 0, "e4m3").reshape(K, 3, J)
    w_ = mxq(f64(w), 0, "e4m3")
    a0 = w_.T @ xT_[:, 0]
    a1 = w_.T @ xT_[:, 1]
    a2 = w_.T @ xT_[:, 2]
    return a0 * f64(iw0) + a1 * f64(iw1) + a2 * f64(iw2) + f64(b)[:, None]

@@ -1,0 +1,159 @@
+from contextlib import ExitStack
+
+import concourse.mybir as mybir
+
+K, N, T, J, PICKS = 512, 512, 2048, 512, 3
+FLOPS = 2 * K * N * J * PICKS
+
+F32 = mybir.dt.float32
+BF16 = mybir.dt.bfloat16
+U32 = mybir.dt.uint32
+U16 = mybir.dt.uint16
+U8 = mybir.dt.uint8
+FP8X4 = mybir.dt.float8_e4m3fn_x4
+MULT = mybir.AluOpType.mult
+ADD = mybir.AluOpType.add
+IDENT = mybir.ActivationFunctionType.Identity
+
+P = 128
+PACK = 4
+HALF = J // 2
+LIST_COLS = HALF // 16
+ADDS = {(0, 0): "VV", (0, 1): "VV", (1, 0): "VV", (1, 1): "VV"}
+
+
+def tile_list_soft_bias_kernel(tc, xT, wgt, w, iw0, iw1, iw2, b, offs, out):
+    nc = tc.nc
+    iw = (iw0, iw1, iw2)
+    with ExitStack() as ctx:
+        keep = ctx.enter_context(tc.tile_pool(name="keep", bufs=1))
+        psum = ctx.enter_context(tc.psum_pool(name="psum", bufs=6))
+
+        offsets = keep.tile([P, PICKS * J // 16], U16, name="offsets")
+        planes = [keep.tile([P, T], F32, name="plane%d" % i) for i in range(PACK)]
+        wgt_0 = keep.tile([P, J], F32, name="wgt_0")
+        wgt_1 = keep.tile([P, HALF], F32, name="wgt_1")
+        wgt_2 = keep.tile([P, HALF], F32, name="wgt_2")
+        wgt_late = keep.tile([P, 2, HALF], F32, name="wgt_late")
+        picked_0 = keep.tile([P, PACK, J], F32, name="picked_0")
+        w_raw = keep.tile([P, PACK, N], F32, name="w_raw")
+        w_bf = keep.tile([P, N, PACK], BF16, name="w_bf", align_bytes=64)
+        w_codes = keep.tile([P, N], U32, name="w_codes", align_bytes=64)
+        w_scales = keep.tile([P, N], U8, name="w_scales", align_bytes=64)
+        bias = keep.tile([P, 4], F32, name="bias")
+        iw_sb = {(c, r): keep.tile([P, 2, J], F32, name="iw%d_%d" % (c, r)) for c in range(PICKS) for r in range(2)}
+        picked, grouped, codes, scales = {}, {}, {}, {}
+        for h in range(2):
+            for c in range(PICKS):
+                if c > 0:
+                    picked[h, c] = keep.tile([P, PACK, HALF], F32, name="picked%d_%d" % (h, c))
+                grouped[h, c] = keep.tile([P, HALF, PACK], BF16, name="grouped%d_%d" % (h, c), align_bytes=64)
+                codes[h, c] = keep.tile([P, HALF], U32, name="codes%d_%d" % (h, c), align_bytes=64)
+                scales[h, c] = keep.tile([P, HALF], U8, name="scales%d_%d" % (h, c), align_bytes=64)
+
+        x_planes = xT.rearrange("(p i) t -> i p t", i=PACK)
+        wgt_v = wgt.rearrange("p (c j) -> p c j", c=PICKS)
+        nc.sync.dma_start(offsets[:], offs)
+        nc.sync.dma_start(out=wgt_1[:], in_=wgt_v[:, 1, 0:HALF])
+        nc.sync.dma_start(out=planes[0][:], in_=x_planes[0])
+        nc.sync.dma_start(out=wgt_2[:], in_=wgt_v[:, 2, 0:HALF])
+        nc.sync.dma_start(out=wgt_0[:], in_=wgt_v[:, 0, :])
+        nc.sync.dma_start(out=planes[1][:], in_=x_planes[1])
+        nc.sync.dma_start(out=planes[2][:], in_=x_planes[2])
+        nc.sync.dma_start(out=planes[3][:], in_=x_planes[3])
+        nc.sync.dma_start(out=wgt_late[:], in_=wgt_v[:, 1:3, HALF:J])
+        nc.sync.dma_start(out=w_raw[:], in_=w.rearrange("(p i) n -> p i n", i=PACK))
+        for r in range(2):
+            for c in range(PICKS):
+                nc.sync.dma_start(out=iw_sb[c, r][:], in_=iw[c][256 * r : 256 * (r + 1), :].rearrange("(s p) j -> p s j", p=P))
+            if r == 0:
+                with nc.allow_non_contiguous_dma(reason="one bias value a partition"):
+                    nc.sync.dma_start(out=bias[:], in_=b.rearrange("(t p) -> p t", p=P))
+
+        def gather(i, h, c):
+            col = (c * 2 + h) * LIST_COLS
+            weights = wgt_late[:, c - 1, :] if h == 1 else (wgt_1, wgt_2)[c - 1][:]
+            nc.vector.tensor_tensor(picked[h, c][:, i, :], planes[i][:].indirect(offsets[:, col : col + LIST_COLS]), weights, MULT)
+
+        def gather_first(i):
+            nc.vector.tensor_tensor(picked_0[:, i, :], planes[i][:].indirect(offsets[:, 0 : 2 * LIST_COLS]), wgt_0[:], MULT)
+
+        def interleave(dst, src):
+            nc.scalar.copy(out=dst[:].rearrange("p (m e) i -> p m i e", e=4), in_=src.rearrange("p i (m e) -> p m i e", e=4))
+
+        def quantize(code, scale, src):
+            nc.vector.quantize_mx(out=code[:].bitcast(FP8X4), scales=scale[:], in_=src[:].rearrange("p j i -> p (j i)"))
+
+        def quantize_x(h, c):
+            quantize(codes[h, c], scales[h, c], grouped[h, c])
+
+        products = {}
+
+        def weigh(h, r, c):
+            acc = psum.tile([P, 2, HALF], F32, name="acc")
+            for s in range(2):
+                cols = slice(P * (2 * r + s), P * (2 * r + s + 1))
+                nc.tensor.matmul_mx(out=acc[:, s, :], lhsT=w_codes[:, cols].bitcast(FP8X4), lhsT_scale=w_scales[:, cols],
+                                    rhs=codes[h, c][:].bitcast(FP8X4), rhs_scale=scales[h, c][:], start=True, stop=True)
+            products[h, r, c] = keep.tile([P, 2, HALF], F32, name="prod%d_%d_%d" % (h, r, c))
+            nc.vector.tensor_tensor(products[h, r, c][:], acc[:], iw_sb[c, r][:, :, h * HALF : (h + 1) * HALF], MULT)
+
+        partial = {}
+
+        def add_first(h, r):
+            partial[h, r] = keep.tile([P, 2, HALF], F32, name="part%d_%d" % (h, r))
+            nc.vector.tensor_tensor(partial[h, r][:], products[h, r, 0][:], products[h, r, 1][:], ADD)
+
+        def add_last(h, r):
+            for s in range(2):
+                t = 2 * r + s
+                res = keep.tile([P, HALF], F32, name="res%d_%d" % (h, t))
+                nc.vector.scalar_tensor_tensor(res[:], products[h, r, 2][:, s, :], bias[:, t : t + 1], partial[h, r][:, s, :], ADD, ADD)
+                nc.sync.dma_start(out=out[P * t : P * (t + 1), h * HALF : (h + 1) * HALF], in_=res[:])
+
+        for i in range(PACK):
+            gather(i, 0, 1)
+            gather(i, 0, 2)
+            gather_first(i)
+        interleave(grouped[0, 1], picked[0, 1][:])
+        interleave(grouped[0, 2], picked[0, 2][:])
+        interleave(grouped[0, 0], picked_0[:, :, 0:HALF])
+        interleave(w_bf, w_raw[:])
+        interleave(grouped[1, 0], picked_0[:, :, HALF:J])
+        gather(0, 1, 1)
+        quantize_x(0, 1)
+        gather(1, 1, 1)
+        gather(2, 1, 1)
+        quantize_x(0, 2)
+        gather(3, 1, 1)
+        interleave(grouped[1, 1], picked[1, 1][:])
+        gather(0, 1, 2)
+        quantize_x(0, 0)
+        gather(1, 1, 2)
+        gather(2, 1, 2)
+        quantize(w_codes, w_scales, w_bf)
+        gather(3, 1, 2)
+        interleave(grouped[1, 2], picked[1, 2][:])
+        quantize_x(1, 0)
+        weigh(0, 0, 0)
+        weigh(0, 0, 1)
+        quantize_x(1, 1)
+        weigh(0, 0, 2)
+        add_first(0, 0)
+        quantize_x(1, 2)
+        weigh(0, 1, 0)
+        add_last(0, 0)
+        weigh(0, 1, 1)
+        weigh(0, 1, 2)
+        add_first(0, 1)
+        weigh(1, 0, 0)
+        add_last(0, 1)
+        weigh(1, 0, 1)
+        weigh(1, 0, 2)
+        add_first(1, 0)
+        weigh(1, 1, 0)
+        add_last(1, 0)
+        weigh(1, 1, 1)
+        weigh(1, 1, 2)
+        add_first(1, 1)
+        add_last(1, 1)

@@ -27,7 +27,7 @@ def tile_list_soft_bias_kernel(tc, xT, wgt, w, iw0, iw1, iw2, b, offs, out):
     iw = (iw0, iw1, iw2)
     with ExitStack() as ctx:
         keep = ctx.enter_context(tc.tile_pool(name="keep", bufs=1))
-        psum = ctx.enter_context(tc.psum_pool(name="psum", bufs=6))
+        psum = ctx.enter_context(tc.psum_pool(name="psum", bufs=8))
 
         offsets = keep.tile([P, PICKS * J // 16], U16, name="offsets")
         planes = [keep.tile([P, T], F32, name="plane%d" % i) for i in range(PACK)]
@@ -100,9 +100,18 @@ def tile_list_soft_bias_kernel(tc, xT, wgt, w, iw0, iw1, iw2, b, offs, out):
 
         partial = {}
 
-        def add_first(h, r):
+        def add_side(h, r):
+            total = keep.tile([P, 2, HALF], F32, name="total%d_%d" % (h, r))
+            nc.gpsimd.tensor_tensor(total[:], partial[h, r][:], products[h, r, 2][:], ADD)
+            res = keep.tile([P, 2, HALF], F32, name="biased%d_%d" % (h, r))
+            for s in range(2):
+                t = 2 * r + s
+                nc.scalar.activation(res[:, s, :], total[:, s, :], IDENT, bias=bias[:, t : t + 1])
+            nc.sync.dma_start(out=out[256 * r : 256 * (r + 1), h * HALF : (h + 1) * HALF].rearrange("(s p) j -> p s j", p=P), in_=res[:])
+
+        def add_first(h, r, engine):
             partial[h, r] = keep.tile([P, 2, HALF], F32, name="part%d_%d" % (h, r))
-            nc.vector.tensor_tensor(partial[h, r][:], products[h, r, 0][:], products[h, r, 1][:], ADD)
+            engine.tensor_tensor(partial[h, r][:], products[h, r, 0][:], products[h, r, 1][:], ADD)
 
         def add_last(h, r):
             for s in range(2):
@@ -120,40 +129,31 @@ def tile_list_soft_bias_kernel(tc, xT, wgt, w, iw0, iw1, iw2, b, offs, out):
         interleave(grouped[0, 0], picked_0[:, :, 0:HALF])
         interleave(w_bf, w_raw[:])
         interleave(grouped[1, 0], picked_0[:, :, HALF:J])
-        gather(0, 1, 1)
+        for c in (1, 2):
+            for i in range(PACK):
+                gather(i, 1, c)
+            interleave(grouped[1, c], picked[1, c][:])
         quantize_x(0, 1)
-        gather(1, 1, 1)
-        gather(2, 1, 1)
         quantize_x(0, 2)
-        gather(3, 1, 1)
-        interleave(grouped[1, 1], picked[1, 1][:])
-        gather(0, 1, 2)
         quantize_x(0, 0)
-        gather(1, 1, 2)
-        gather(2, 1, 2)
         quantize(w_codes, w_scales, w_bf)
-        gather(3, 1, 2)
-        interleave(grouped[1, 2], picked[1, 2][:])
         quantize_x(1, 0)
-        weigh(0, 0, 0)
-        weigh(0, 0, 1)
         quantize_x(1, 1)
-        weigh(0, 0, 2)
-        add_first(0, 0)
+        weigh(0, 0, 0)
         quantize_x(1, 2)
+        weigh(0, 0, 1)
+        add_first(0, 0, nc.gpsimd)
+        weigh(0, 0, 2)
+        add_side(0, 0)
         weigh(0, 1, 0)
-        add_last(0, 0)
         weigh(0, 1, 1)
+        add_first(0, 1, nc.gpsimd)
         weigh(0, 1, 2)
-        add_first(0, 1)
-        weigh(1, 0, 0)
-        add_last(0, 1)
-        weigh(1, 0, 1)
-        weigh(1, 0, 2)
-        add_first(1, 0)
-        weigh(1, 1, 0)
+        add_side(0, 1)
+        for r in range(2):
+            for c in range(PICKS):
+                weigh(1, r, c)
+        add_first(1, 0, nc.vector)
+        add_first(1, 1, nc.vector)
         add_last(1, 0)
-        weigh(1, 1, 1)
-        weigh(1, 1, 2)
-        add_first(1, 1)
         add_last(1, 1)

@@ -1,6 +1,7 @@
 from contextlib import ExitStack
 
 import concourse.mybir as mybir
+from concourse.masks import make_identity
 
 K, N, T, J, PICKS = 512, 512, 2048, 512, 3
 FLOPS = 2 * K * N * J * PICKS
@@ -18,8 +19,8 @@ IDENT = mybir.ActivationFunctionType.Identity
 P = 128
 PACK = 4
 HALF = J // 2
-LIST_COLS = HALF // 16
-ADDS = {(0, 0): "VV", (0, 1): "VV", (1, 0): "VV", (1, 1): "VV"}
+ROW_TILES = N // P
+ORDER = [(0, 0), (0, 1), (1, 0), (1, 1), (2, 0), (0, 2), (2, 1), (3, 0), (3, 1), (1, 2), (2, 2), (3, 2)]
 
 
 def tile_list_soft_bias_kernel(tc, xT, wgt, w, iw0, iw1, iw2, b, offs, out):
@@ -27,133 +28,122 @@ def tile_list_soft_bias_kernel(tc, xT, wgt, w, iw0, iw1, iw2, b, offs, out):
     iw = (iw0, iw1, iw2)
     with ExitStack() as ctx:
         keep = ctx.enter_context(tc.tile_pool(name="keep", bufs=1))
-        psum = ctx.enter_context(tc.psum_pool(name="psum", bufs=8))
+        psum = ctx.enter_context(tc.psum_pool(name="psum", bufs=4))
+        turn = ctx.enter_context(tc.psum_pool(name="turn", bufs=2))
 
         offsets = keep.tile([P, PICKS * J // 16], U16, name="offsets")
         planes = [keep.tile([P, T], F32, name="plane%d" % i) for i in range(PACK)]
-        wgt_0 = keep.tile([P, J], F32, name="wgt_0")
-        wgt_1 = keep.tile([P, HALF], F32, name="wgt_1")
-        wgt_2 = keep.tile([P, HALF], F32, name="wgt_2")
-        wgt_late = keep.tile([P, 2, HALF], F32, name="wgt_late")
-        picked_0 = keep.tile([P, PACK, J], F32, name="picked_0")
+        wgt_sb = keep.tile([P, PICKS, J], F32, name="wgt_sb")
+        picked = [keep.tile([P, PACK, J], F32, name="picked%d" % c) for c in range(PICKS)]
+        grouped = [keep.tile([P, J, PACK], BF16, name="grouped%d" % c, align_bytes=64) for c in range(2)]
+        last_a = keep.tile([P, HALF, PACK], BF16, name="last_a", tag="last_a", align_bytes=64)
+        last_b = keep.tile([P, HALF, PACK], BF16, name="last_b", tag="last_b", align_bytes=64)
         w_raw = keep.tile([P, PACK, N], F32, name="w_raw")
         w_bf = keep.tile([P, N, PACK], BF16, name="w_bf", align_bytes=64)
         w_codes = keep.tile([P, N], U32, name="w_codes", align_bytes=64)
         w_scales = keep.tile([P, N], U8, name="w_scales", align_bytes=64)
-        bias = keep.tile([P, 4], F32, name="bias")
-        iw_sb = {(c, r): keep.tile([P, 2, J], F32, name="iw%d_%d" % (c, r)) for c in range(PICKS) for r in range(2)}
-        picked, grouped, codes, scales = {}, {}, {}, {}
-        for h in range(2):
-            for c in range(PICKS):
-                if c > 0:
-                    picked[h, c] = keep.tile([P, PACK, HALF], F32, name="picked%d_%d" % (h, c))
-                grouped[h, c] = keep.tile([P, HALF, PACK], BF16, name="grouped%d_%d" % (h, c), align_bytes=64)
-                codes[h, c] = keep.tile([P, HALF], U32, name="codes%d_%d" % (h, c), align_bytes=64)
-                scales[h, c] = keep.tile([P, HALF], U8, name="scales%d_%d" % (h, c), align_bytes=64)
+        codes = [keep.tile([P, J], U32, name="codes%d" % c, align_bytes=64) for c in range(PICKS)]
+        scales = [keep.tile([P, J], U8, name="scales%d" % c, align_bytes=64) for c in range(PICKS)]
+        bias = keep.tile([P, ROW_TILES], F32, name="bias")
+        iw_sb = {(t, c): keep.tile([P, J], F32, name="iw%d_%d" % (t, c)) for t, c in ORDER}
+        identity = keep.tile([P, P], F32, name="identity")
+        make_identity(nc, identity[:])
 
         x_planes = xT.rearrange("(p i) t -> i p t", i=PACK)
-        wgt_v = wgt.rearrange("p (c j) -> p c j", c=PICKS)
+        wgt_flat = wgt_sb[:].rearrange("p c j -> p (c j)")
         nc.sync.dma_start(offsets[:], offs)
-        nc.sync.dma_start(out=wgt_1[:], in_=wgt_v[:, 1, 0:HALF])
+        nc.sync.dma_start(out=wgt_flat[:, 0:HALF], in_=wgt[:, 0:HALF])
         nc.sync.dma_start(out=planes[0][:], in_=x_planes[0])
-        nc.sync.dma_start(out=wgt_2[:], in_=wgt_v[:, 2, 0:HALF])
-        nc.sync.dma_start(out=wgt_0[:], in_=wgt_v[:, 0, :])
-        nc.sync.dma_start(out=planes[1][:], in_=x_planes[1])
-        nc.sync.dma_start(out=planes[2][:], in_=x_planes[2])
-        nc.sync.dma_start(out=planes[3][:], in_=x_planes[3])
-        nc.sync.dma_start(out=wgt_late[:], in_=wgt_v[:, 1:3, HALF:J])
+        nc.sync.dma_start(out=wgt_flat[:, HALF:J], in_=wgt[:, HALF:J])
+        nc.sync.dma_start(out=wgt_sb[:, 1, :], in_=wgt[:, J : 2 * J])
+        for i in range(1, PACK):
+            nc.sync.dma_start(out=planes[i][:], in_=x_planes[i])
+        nc.sync.dma_start(out=wgt_sb[:, 2, :], in_=wgt[:, 2 * J : 3 * J])
         nc.sync.dma_start(out=w_raw[:], in_=w.rearrange("(p i) n -> p i n", i=PACK))
-        for r in range(2):
-            for c in range(PICKS):
-                nc.sync.dma_start(out=iw_sb[c, r][:], in_=iw[c][256 * r : 256 * (r + 1), :].rearrange("(s p) j -> p s j", p=P))
-            if r == 0:
-                with nc.allow_non_contiguous_dma(reason="one bias value a partition"):
-                    nc.sync.dma_start(out=bias[:], in_=b.rearrange("(t p) -> p t", p=P))
+        with nc.allow_non_contiguous_dma(reason="one bias value a partition"):
+            nc.sync.dma_start(out=bias[:], in_=b.rearrange("(t p) -> p t", p=P))
+        for t, c in ORDER:
+            nc.sync.dma_start(out=iw_sb[t, c][:], in_=iw[c][P * t : P * (t + 1), :])
 
-        def gather(i, h, c):
-            col = (c * 2 + h) * LIST_COLS
-            weights = wgt_late[:, c - 1, :] if h == 1 else (wgt_1, wgt_2)[c - 1][:]
-            nc.vector.tensor_tensor(picked[h, c][:, i, :], planes[i][:].indirect(offsets[:, col : col + LIST_COLS]), weights, MULT)
-
-        def gather_first(i):
-            nc.vector.tensor_tensor(picked_0[:, i, :], planes[i][:].indirect(offsets[:, 0 : 2 * LIST_COLS]), wgt_0[:], MULT)
+        def gather(i, c, lo, hi):
+            entries = offsets[:, (c * J + lo) // 16 : (c * J + hi) // 16]
+            nc.vector.tensor_tensor(picked[c][:, i, lo:hi], planes[i][:].indirect(entries), wgt_sb[:, c, lo:hi], MULT)
 
         def interleave(dst, src):
-            nc.scalar.copy(out=dst[:].rearrange("p (m e) i -> p m i e", e=4), in_=src.rearrange("p i (m e) -> p m i e", e=4))
+            nc.scalar.copy(out=dst.rearrange("p (m e) i -> p m i e", e=4), in_=src.rearrange("p i (m e) -> p m i e", e=4))
 
         def quantize(code, scale, src):
-            nc.vector.quantize_mx(out=code[:].bitcast(FP8X4), scales=scale[:], in_=src[:].rearrange("p j i -> p (j i)"))
+            nc.vector.quantize_mx(out=code.bitcast(FP8X4), scales=scale, in_=src[:].rearrange("p j i -> p (j i)"))
 
-        def quantize_x(h, c):
-            quantize(codes[h, c], scales[h, c], grouped[h, c])
-
-        products = {}
-
-        def weigh(h, r, c):
-            acc = psum.tile([P, 2, HALF], F32, name="acc")
-            for s in range(2):
-                cols = slice(P * (2 * r + s), P * (2 * r + s + 1))
-                nc.tensor.matmul_mx(out=acc[:, s, :], lhsT=w_codes[:, cols].bitcast(FP8X4), lhsT_scale=w_scales[:, cols],
-                                    rhs=codes[h, c][:].bitcast(FP8X4), rhs_scale=scales[h, c][:], start=True, stop=True)
-            products[h, r, c] = keep.tile([P, 2, HALF], F32, name="prod%d_%d_%d" % (h, r, c))
-            nc.vector.tensor_tensor(products[h, r, c][:], acc[:], iw_sb[c, r][:, :, h * HALF : (h + 1) * HALF], MULT)
-
-        partial = {}
-
-        def add_side(h, r):
-            total = keep.tile([P, 2, HALF], F32, name="total%d_%d" % (h, r))
-            nc.gpsimd.tensor_tensor(total[:], partial[h, r][:], products[h, r, 2][:], ADD)
-            res = keep.tile([P, 2, HALF], F32, name="biased%d_%d" % (h, r))
-            for s in range(2):
-                t = 2 * r + s
-                nc.scalar.activation(res[:, s, :], total[:, s, :], IDENT, bias=bias[:, t : t + 1])
-            nc.sync.dma_start(out=out[256 * r : 256 * (r + 1), h * HALF : (h + 1) * HALF].rearrange("(s p) j -> p s j", p=P), in_=res[:])
-
-        def add_first(h, r, engine):
-            partial[h, r] = keep.tile([P, 2, HALF], F32, name="part%d_%d" % (h, r))
-            engine.tensor_tensor(partial[h, r][:], products[h, r, 0][:], products[h, r, 1][:], ADD)
-
-        def add_last(h, r):
-            for s in range(2):
-                t = 2 * r + s
-                res = keep.tile([P, HALF], F32, name="res%d_%d" % (h, t))
-                nc.vector.scalar_tensor_tensor(res[:], products[h, r, 2][:, s, :], bias[:, t : t + 1], partial[h, r][:, s, :], ADD, ADD)
-                nc.sync.dma_start(out=out[P * t : P * (t + 1), h * HALF : (h + 1) * HALF], in_=res[:])
-
+        gather(0, 0, 0, HALF)
+        gather(0, 0, HALF, J)
+        gather(0, 1, 0, J)
+        for i in range(1, PACK - 1):
+            gather(i, 0, 0, J)
+            gather(i, 1, 0, J)
+        gather(PACK - 1, 0, 0, HALF)
+        gather(PACK - 1, 0, HALF, J)
+        gather(PACK - 1, 1, 0, J)
+        interleave(grouped[0][:, 0:HALF, :], picked[0][:, :, 0:HALF])
+        interleave(grouped[0][:, HALF:J, :], picked[0][:, :, HALF:J])
+        interleave(grouped[1][:], picked[1][:])
+        interleave(w_bf[:], w_raw[:])
         for i in range(PACK):
-            gather(i, 0, 1)
-            gather(i, 0, 2)
-            gather_first(i)
-        interleave(grouped[0, 1], picked[0, 1][:])
-        interleave(grouped[0, 2], picked[0, 2][:])
-        interleave(grouped[0, 0], picked_0[:, :, 0:HALF])
-        interleave(w_bf, w_raw[:])
-        interleave(grouped[1, 0], picked_0[:, :, HALF:J])
-        for c in (1, 2):
-            for i in range(PACK):
-                gather(i, 1, c)
-            interleave(grouped[1, c], picked[1, c][:])
-        quantize_x(0, 1)
-        quantize_x(0, 2)
-        quantize_x(0, 0)
-        quantize(w_codes, w_scales, w_bf)
-        quantize_x(1, 0)
-        quantize_x(1, 1)
-        weigh(0, 0, 0)
-        quantize_x(1, 2)
-        weigh(0, 0, 1)
-        add_first(0, 0, nc.gpsimd)
-        weigh(0, 0, 2)
-        add_side(0, 0)
-        weigh(0, 1, 0)
-        weigh(0, 1, 1)
-        add_first(0, 1, nc.gpsimd)
-        weigh(0, 1, 2)
-        add_side(0, 1)
-        for r in range(2):
-            for c in range(PICKS):
-                weigh(1, r, c)
-        add_first(1, 0, nc.vector)
-        add_first(1, 1, nc.vector)
-        add_last(1, 0)
-        add_last(1, 1)
+            gather(i, 2, 0, J)
+        interleave(last_a[:], picked[2][:, :, 0:HALF])
+        interleave(last_b[:], picked[2][:, :, HALF:J])
+        for c in range(2):
+            quantize(codes[c][:], scales[c][:], grouped[c])
+        quantize(w_codes[:], w_scales[:], w_bf)
+        quantize(codes[2][:, 0:HALF], scales[2][:, 0:HALF], last_a)
+        quantize(codes[2][:, HALF:J], scales[2][:, HALF:J], last_b)
+
+        products = keep.tile([P, ROW_TILES, PICKS, J], F32, name="products", tag="last_a", align_bytes=64)
+        partial = keep.tile([P, 2, J], F32, name="partial", tag="last_b", align_bytes=64)
+        back, biased = {}, {}
+
+        def weigh(t, c):
+            acc = psum.tile([P, J], F32, name="acc")
+            cols = slice(P * t, P * (t + 1))
+            nc.tensor.matmul_mx(out=acc[:], lhsT=w_codes[:, cols].bitcast(FP8X4), lhsT_scale=w_scales[:, cols],
+                                rhs=codes[c][:].bitcast(FP8X4), rhs_scale=scales[c][:], start=True, stop=True)
+            nc.vector.tensor_tensor(products[:, t, c, :], acc[:], iw_sb[t, c][:], MULT)
+
+        def pair_on_gpsimd(t):
+            nc.gpsimd.tensor_tensor(partial[:, t, :], products[:, t, 0, :], products[:, t, 1, :], ADD)
+            biased[t] = keep.tile([P, J], F32, name="biased%d" % t)
+            nc.scalar.activation(biased[t][:], partial[:, t, :], IDENT, bias=bias[:, t : t + 1])
+
+        def finish_on_gpsimd(t):
+            res = keep.tile([P, J], F32, name="total%d" % t)
+            nc.gpsimd.tensor_tensor(res[:], biased[t][:], products[:, t, 2, :], ADD)
+            nc.sync.dma_start(out=out[P * t : P * (t + 1), :], in_=res[:])
+
+        def pair_on_tensor(t):
+            turned = turn.tile([P, 4, P], F32, name="turned")
+            for c in range(2):
+                for q in range(4):
+                    nc.tensor.matmul(turned[:, q, :], products[:, t, c, P * q : P * (q + 1)], identity[:],
+                                     start=(c == 0 and q == 0), stop=(c == 1 and q == 3), is_transpose=True)
+            turned_sb = keep.tile([P, 4, P], F32, name="turned_sb%d" % t)
+            nc.scalar.copy(out=turned_sb[:], in_=turned[:])
+            back[t] = turn.tile([P, J], F32, name="back")
+            for q in range(4):
+                nc.tensor.transpose(back[t][:, P * q : P * (q + 1)], turned_sb[:, q, :], identity[:])
+
+        def finish_on_vector(t, lo, hi):
+            res = keep.tile([P, hi - lo], F32, name="res%d_%d" % (t, lo))
+            nc.vector.scalar_tensor_tensor(res[:], back[t][:, lo:hi], bias[:, t : t + 1], products[:, t, 2, lo:hi], ADD, ADD)
+            nc.sync.dma_start(out=out[P * t : P * (t + 1), lo:hi], in_=res[:])
+
+        for t, c in ORDER:
+            weigh(t, c)
+            if t < 2 and c == 1:
+                pair_on_gpsimd(t)
+            if t < 2 and c == 2:
+                finish_on_gpsimd(t)
+            if t >= 2 and c == 1:
+                pair_on_tensor(t)
+        finish_on_vector(2, 0, J)
+        finish_on_vector(3, 0, HALF)
+        finish_on_vector(3, HALF, J)

@@ -20,7 +20,7 @@ P = 128
 PACK = 4
 HALF = J // 2
 ROW_TILES = N // P
-ORDER = [(0, 0), (0, 1), (1, 0), (1, 1), (2, 0), (0, 2), (2, 1), (3, 0), (3, 1), (1, 2), (2, 2), (3, 2)]
+ORDER = [(0, 0), (0, 1), (2, 0), (2, 1), (1, 0), (1, 1), (0, 2), (3, 0), (3, 1), (1, 2), (2, 2), (3, 2)]
 
 
 def tile_list_soft_bias_kernel(tc, xT, wgt, w, iw0, iw1, iw2, b, offs, out):
@@ -144,6 +144,7 @@ def tile_list_soft_bias_kernel(tc, xT, wgt, w, iw0, iw1, iw2, b, offs, out):
                 finish_on_gpsimd(t)
             if t >= 2 and c == 1:
                 pair_on_tensor(t)
-        finish_on_vector(2, 0, J)
+            if (t, c) == (2, 2):
+                finish_on_vector(t, 0, J)
         finish_on_vector(3, 0, HALF)
         finish_on_vector(3, HALF, J)

from contextlib import ExitStack

import concourse.mybir as mybir
from concourse.masks import make_identity

K, N, T, J, PICKS = 512, 512, 2048, 512, 3
FLOPS = 2 * K * N * J * PICKS

F32 = mybir.dt.float32
BF16 = mybir.dt.bfloat16
U32 = mybir.dt.uint32
U16 = mybir.dt.uint16
U8 = mybir.dt.uint8
FP8X4 = mybir.dt.float8_e4m3fn_x4
MULT = mybir.AluOpType.mult
ADD = mybir.AluOpType.add
IDENT = mybir.ActivationFunctionType.Identity

P = 128
PACK = 4
HALF = J // 2
ROW_TILES = N // P
ORDER = [(0, 0), (0, 1), (2, 0), (2, 1), (1, 0), (1, 1), (0, 2), (3, 0), (3, 1), (1, 2), (2, 2), (3, 2)]


def tile_list_soft_bias_kernel(tc, xT, wgt, w, iw0, iw1, iw2, b, offs, out):
    nc = tc.nc
    iw = (iw0, iw1, iw2)
    with ExitStack() as ctx:
        keep = ctx.enter_context(tc.tile_pool(name="keep", bufs=1))
        psum = ctx.enter_context(tc.psum_pool(name="psum", bufs=4))
        turn = ctx.enter_context(tc.psum_pool(name="turn", bufs=2))

        offsets = keep.tile([P, PICKS * J // 16], U16, name="offsets")
        planes = [keep.tile([P, T], F32, name="plane%d" % i) for i in range(PACK)]
        wgt_sb = keep.tile([P, PICKS, J], F32, name="wgt_sb")
        picked = [keep.tile([P, PACK, J], F32, name="picked%d" % c) for c in range(PICKS)]
        grouped = [keep.tile([P, J, PACK], BF16, name="grouped%d" % c, align_bytes=64) for c in range(2)]
        last_a = keep.tile([P, HALF, PACK], BF16, name="last_a", tag="last_a", align_bytes=64)
        last_b = keep.tile([P, HALF, PACK], BF16, name="last_b", tag="last_b", align_bytes=64)
        w_raw = keep.tile([P, PACK, N], F32, name="w_raw")
        w_bf = keep.tile([P, N, PACK], BF16, name="w_bf", align_bytes=64)
        w_codes = keep.tile([P, N], U32, name="w_codes", align_bytes=64)
        w_scales = keep.tile([P, N], U8, name="w_scales", align_bytes=64)
        codes = [keep.tile([P, J], U32, name="codes%d" % c, align_bytes=64) for c in range(PICKS)]
        scales = [keep.tile([P, J], U8, name="scales%d" % c, align_bytes=64) for c in range(PICKS)]
        bias = keep.tile([P, ROW_TILES], F32, name="bias")
        iw_sb = {(t, c): keep.tile([P, J], F32, name="iw%d_%d" % (t, c)) for t, c in ORDER}
        identity = keep.tile([P, P], F32, name="identity")
        make_identity(nc, identity[:])

        x_planes = xT.rearrange("(p i) t -> i p t", i=PACK)
        wgt_flat = wgt_sb[:].rearrange("p c j -> p (c j)")
        nc.sync.dma_start(offsets[:], offs)
        nc.sync.dma_start(out=wgt_flat[:, 0:HALF], in_=wgt[:, 0:HALF])
        nc.sync.dma_start(out=planes[0][:], in_=x_planes[0])
        nc.sync.dma_start(out=wgt_flat[:, HALF:J], in_=wgt[:, HALF:J])
        nc.sync.dma_start(out=wgt_sb[:, 1, :], in_=wgt[:, J : 2 * J])
        for i in range(1, PACK):
            nc.sync.dma_start(out=planes[i][:], in_=x_planes[i])
        nc.sync.dma_start(out=wgt_sb[:, 2, :], in_=wgt[:, 2 * J : 3 * J])
        nc.sync.dma_start(out=w_raw[:], in_=w.rearrange("(p i) n -> p i n", i=PACK))
        with nc.allow_non_contiguous_dma(reason="one bias value a partition"):
            nc.sync.dma_start(out=bias[:], in_=b.rearrange("(t p) -> p t", p=P))
        for t, c in ORDER:
            nc.sync.dma_start(out=iw_sb[t, c][:], in_=iw[c][P * t : P * (t + 1), :])

        def gather(i, c, lo, hi):
            entries = offsets[:, (c * J + lo) // 16 : (c * J + hi) // 16]
            nc.vector.tensor_tensor(picked[c][:, i, lo:hi], planes[i][:].indirect(entries), wgt_sb[:, c, lo:hi], MULT)

        def interleave(dst, src):
            nc.scalar.copy(out=dst.rearrange("p (m e) i -> p m i e", e=4), in_=src.rearrange("p i (m e) -> p m i e", e=4))

        def quantize(code, scale, src):
            nc.vector.quantize_mx(out=code.bitcast(FP8X4), scales=scale, in_=src[:].rearrange("p j i -> p (j i)"))

        gather(0, 0, 0, HALF)
        gather(0, 0, HALF, J)
        gather(0, 1, 0, J)
        for i in range(1, PACK - 1):
            gather(i, 0, 0, J)
            gather(i, 1, 0, J)
        gather(PACK - 1, 0, 0, HALF)
        gather(PACK - 1, 0, HALF, J)
        gather(PACK - 1, 1, 0, J)
        interleave(grouped[0][:, 0:HALF, :], picked[0][:, :, 0:HALF])
        interleave(grouped[0][:, HALF:J, :], picked[0][:, :, HALF:J])
        interleave(grouped[1][:], picked[1][:])
        interleave(w_bf[:], w_raw[:])
        for i in range(PACK):
            gather(i, 2, 0, J)
        interleave(last_a[:], picked[2][:, :, 0:HALF])
        interleave(last_b[:], picked[2][:, :, HALF:J])
        for c in range(2):
            quantize(codes[c][:], scales[c][:], grouped[c])
        quantize(w_codes[:], w_scales[:], w_bf)
        quantize(codes[2][:, 0:HALF], scales[2][:, 0:HALF], last_a)
        quantize(codes[2][:, HALF:J], scales[2][:, HALF:J], last_b)

        products = keep.tile([P, ROW_TILES, PICKS, J], F32, name="products", tag="last_a", align_bytes=64)
        partial = keep.tile([P, 2, J], F32, name="partial", tag="last_b", align_bytes=64)
        back, biased = {}, {}

        def weigh(t, c):
            acc = psum.tile([P, J], F32, name="acc")
            cols = slice(P * t, P * (t + 1))
            nc.tensor.matmul_mx(out=acc[:], lhsT=w_codes[:, cols].bitcast(FP8X4), lhsT_scale=w_scales[:, cols],
                                rhs=codes[c][:].bitcast(FP8X4), rhs_scale=scales[c][:], start=True, stop=True)
            nc.vector.tensor_tensor(products[:, t, c, :], acc[:], iw_sb[t, c][:], MULT)

        def pair_on_gpsimd(t):
            nc.gpsimd.tensor_tensor(partial[:, t, :], products[:, t, 0, :], products[:, t, 1, :], ADD)
            biased[t] = keep.tile([P, J], F32, name="biased%d" % t)
            nc.scalar.activation(biased[t][:], partial[:, t, :], IDENT, bias=bias[:, t : t + 1])

        def finish_on_gpsimd(t):
            res = keep.tile([P, J], F32, name="total%d" % t)
            nc.gpsimd.tensor_tensor(res[:], biased[t][:], products[:, t, 2, :], ADD)
            nc.sync.dma_start(out=out[P * t : P * (t + 1), :], in_=res[:])

        def pair_on_tensor(t):
            turned = turn.tile([P, 4, P], F32, name="turned")
            for c in range(2):
                for q in range(4):
                    nc.tensor.matmul(turned[:, q, :], products[:, t, c, P * q : P * (q + 1)], identity[:],
                                     start=(c == 0 and q == 0), stop=(c == 1 and q == 3), is_transpose=True)
            turned_sb = keep.tile([P, 4, P], F32, name="turned_sb%d" % t)
            nc.scalar.copy(out=turned_sb[:], in_=turned[:])
            back[t] = turn.tile([P, J], F32, name="back")
            for q in range(4):
                nc.tensor.transpose(back[t][:, P * q : P * (q + 1)], turned_sb[:, q, :], identity[:])

        def finish_on_vector(t, lo, hi):
            res = keep.tile([P, hi - lo], F32, name="res%d_%d" % (t, lo))
            nc.vector.scalar_tensor_tensor(res[:], back[t][:, lo:hi], bias[:, t : t + 1], products[:, t, 2, lo:hi], ADD, ADD)
            nc.sync.dma_start(out=out[P * t : P * (t + 1), lo:hi], in_=res[:])

        for t, c in ORDER:
            weigh(t, c)
            if t < 2 and c == 1:
                pair_on_gpsimd(t)
            if t < 2 and c == 2:
                finish_on_gpsimd(t)
            if t >= 2 and c == 1:
                pair_on_tensor(t)
            if (t, c) == (2, 2):
                finish_on_vector(t, 0, J)
        finish_on_vector(3, 0, HALF)
        finish_on_vector(3, HALF, J)
